import numpy as np
import ml_dtypes


def mxq(x, axis, fmt="e4m3"):
    dtype, down = {"e4m3": (ml_dtypes.float8_e4m3fn, 7), "e5m2": (ml_dtypes.float8_e5m2, 14)}[fmt]
    v = np.moveaxis(np.asarray(x, np.float32).astype(ml_dtypes.bfloat16).astype(np.float64), axis, -1)
    blocks = v.reshape(v.shape[:-1] + (-1, 32))
    amax = np.abs(blocks).max(-1, keepdims=True)
    byte = np.maximum(np.where(amax > 0, np.frexp(amax)[1] - 1 + 127, 0) - down, 1)
    scale = np.exp2(byte - 127.0)
    codes = (blocks / scale).astype(np.float32).astype(dtype).astype(np.float64)
    return np.moveaxis((codes * scale).reshape(v.shape), -1, axis)


WIDE = False


def mx_kscale(k):
    if not WIDE:
        return np.ones(k)
    levels = np.array([10, -10, 5, -5, 0])
    if k % 512:
        return np.exp2(np.random.permutation(np.resize(levels, k // 32))).repeat(32)
    a = np.empty((k // 512, 16))
    for p in range(k // 512):
        a[p, :8] = np.random.permutation(np.resize(levels, 8))
        for g in range(8):
            far = levels[np.abs(levels - a[p, g]) >= 10]
            a[p, g + 8] = far[np.random.randint(len(far))]
    return np.exp2(a.ravel()).repeat(32)


BF16 = ml_dtypes.bfloat16


def bf(x):
    return np.asarray(x, np.float32).astype(BF16)


def f64(x):
    return np.asarray(x).astype(np.float64)


B, K, T, D, N = 512, 1024, 1024, 512, 2048


def draw0():
    s = mx_kscale(K)
    u = mx_kscale(D)
    t = mx_kscale(T)
    queries = np.random.standard_normal((B, K)) * s
    w = np.random.standard_normal((K, T)) / np.sqrt(K) * T ** -0.25 / s[:, None] * t
    b = 0.1 * np.random.standard_normal(T) * t
    terms = np.random.standard_normal((T, D)) / np.sqrt(D) * u / t[:, None]
    c = 0.3 * np.random.standard_normal(T) / t
    docs = np.random.standard_normal((N, D)) / u
    return {"queries": bf(queries), "w": bf(w), "b": bf(b),
            "terms": bf(terms), "c": bf(c), "docs": bf(docs)}


def core(queries, w, b, terms, c, docs):
    r = (mxq(f64(queries), 1, "e4m3") @ mxq(f64(w), 0, "e4m3")) + f64(b)
    m = mxq(f64(terms), 1, "e4m3") @ mxq(f64(docs), 1, "e4m3").T
    m = np.maximum(m + f64(c)[:, None], 0.0)
    return mxq(r, 1, "e4m3") @ mxq(m, 0, "e4m3")


def e4m3fn_bytes(y):
    return np.clip(np.asarray(y, np.float64), -448.0, 448.0).astype(np.float32).astype(ml_dtypes.float8_e4m3fn).view(np.uint8)


def e4m3fn_values(b):
    return np.asarray(b, np.uint8).view(ml_dtypes.float8_e4m3fn).astype(np.float64)


def setup_inputs():
    d = draw0()
    x0 = np.asarray(d['docs']).astype(np.float64)
    s = (np.max(np.abs(x0), axis=(0,), keepdims=True) / 448.0).astype(np.float32)
    out = {}
    for k, v in d.items():
        if k == 'docs':
            out['docs_bytes'] = e4m3fn_bytes(x0 / s.astype(np.float64))
            out['docs_scale'] = s
        else:
            out[k] = v
    return out


def reference(queries, w, b, terms, c, docs_bytes, docs_scale):
    return core(queries, w, b, terms, c, e4m3fn_values(docs_bytes) * docs_scale.astype(np.float64))

@@ -1,0 +1,278 @@
+from contextlib import ExitStack
+
+import concourse.mybir as mybir
+from concourse.masks import make_identity
+
+B, K, T, D, N = 512, 1024, 1024, 512, 2048
+FLOPS = 2 * (B * K * T + T * D * N + B * T * N)
+
+F32 = mybir.dt.float32
+BF16 = mybir.dt.bfloat16
+U32 = mybir.dt.uint32
+U8 = mybir.dt.uint8
+FP8 = mybir.dt.float8_e4m3fn
+FP8X4 = mybir.dt.float8_e4m3fn_x4
+ACT = mybir.ActivationFunctionType
+ALU = mybir.AluOpType
+
+LOADS = [
+    "d00", "d01", "q0", "d1", "d2", "w10", "t1", "t00", "w11", "q1",
+    "w00", "t01", "w01", "d3",
+]
+ORDER = [
+    "P_00", "Tq00:s", "Td00:s", "Tq01:s", "P_01", "P_10", "P_11",
+    "Iw10:s", "Tt00:s", "P_20", "Tt10:s", "P_21", "Td11:s", "Td01:s",
+    "Qq0", "Iw11:v", "Qd0", "Tq10:s", "Iw00:v", "Tt11:s", "Td10:s",
+    "Td21:s", "Tq11:s", "Tt01:s", "Qt1", "Td20:s", "Iw01:v", "Qt0",
+    "Qq1", "M_01:ssss", "M_00:ssss", "Qw10", "Qw01", "Qw00", "R_0:ssss",
+    "P_30", "Qd1", "Qw11", "Gm00", "Qd2", "Td30:v", "Gm01", "P_31",
+    "R_1:ssss", "Gr1", "M_10:ssss", "Gr0", "Td31:s", "M_11:ssvs",
+    "Qm00", "Qm01", "M_20:ssss", "Qd3", "Qr1", "Qr0", "Gm10", "M_21:ssss",
+    "Gm20", "Qm10", "S_0:svss", "Gm11", "Gm21", "Qm11", "Qm20", "M_31:ssss",
+    "M_30:svss", "Qm21", "Gm30", "Gh311", "S_1:ssss", "Qm30", "S_2:ssss",
+    "Qh311", "Sh31:ssss", "Gh310", "Qh310", "Sh30:svss",
+]
+PL = 5
+
+P = 128
+W = 512
+
+
+def tile_query_rewrite_scoring_s7_kernel(
+    tc, queries, w, b, terms, c, docs_bytes, docs_scale, out
+):
+    nc = tc.nc
+    with ExitStack() as ctx:
+        keep = ctx.enter_context(tc.tile_pool(name="keep", bufs=1))
+        ring = ctx.enter_context(tc.tile_pool(name="ring", bufs=3))
+        psum = ctx.enter_context(tc.psum_pool(name="psum", bufs=8))
+        ctx.enter_context(tc.manual_schedule())
+
+        def bank():
+            return psum.tile([P, W], F32, name="bank")
+
+        def codes(name):
+            return (
+                keep.tile([P, W], U32, name=name + "_codes", align_bytes=64),
+                keep.tile([P, W], U8, name=name + "_scales", align_bytes=64),
+            )
+
+        ident = keep.tile([P, P], F32, name="ident")
+        bias_raw = [keep.tile([P, 2, 4], BF16, name=f"bias_raw{s}") for s in range(2)]
+        bias = keep.tile([P, 2, 2, 4], F32, name="bias")
+        warm = keep.tile([P, 2], F32, name="warm")
+        scale = keep.tile([P, D], F32, name="scale")
+        scale2 = keep.tile([P, 2, D], F32, name="scale2")
+        x_docs = [keep.tile([P, 4 * D], U8, name=f"x_docs{i}") for i in range(4)]
+        v_docs = [keep.tile([P, 4 * D], BF16, name=f"v_docs{i}") for i in range(4)]
+        x_terms = [keep.tile([P, 4 * D], BF16, name=f"x_terms{g}") for g in range(2)]
+        x_q = [keep.tile([P, 4, 512], BF16, name=f"x_q{h}") for h in range(2)]
+        x_w = [[keep.tile([P, 4, W], BF16, name=f"x_w{h}{g}") for g in range(2)] for h in range(2)]
+        g_docs = [keep.tile([P, W, 4], BF16, name=f"g_docs{i}", align_bytes=64) for i in range(4)]
+        g_terms = [keep.tile([P, W, 4], BF16, name=f"g_terms{g}", align_bytes=64) for g in range(2)]
+        g_q = [keep.tile([P, W, 4], BF16, name=f"g_q{h}", align_bytes=64) for h in range(2)]
+        g_w = [[keep.tile([P, W * 4], BF16, name=f"g_w{h}{g}", align_bytes=64) for g in range(2)] for h in range(2)]
+        q_docs = [codes(f"q_docs{i}") for i in range(4)]
+        q_terms = [codes(f"q_terms{g}") for g in range(2)]
+        q_q = [codes(f"q_q{h}") for h in range(2)]
+        q_w = [[codes(f"q_w{h}{g}") for g in range(2)] for h in range(2)]
+        q_r = [codes(f"q_r{g}") for g in range(2)]
+        q_m = [[codes(f"q_m{i}{g}") for g in range(2)] for i in range(4)]
+
+        docs_v = docs_bytes.rearrange("(i m s) k -> i m (s k)", i=4, s=4)
+        terms_v = terms.rearrange("(g m j) k -> g m (j k)", g=2, j=4)
+        q_v = queries.rearrange("(m r) (h k) -> h m r k", r=4, h=2)
+        w_v = w.rearrange("(h p j) (g c) -> h g p j c", h=2, j=4, g=2)
+        out_v = out.rearrange("(m r) n -> r m n", r=4)
+
+        nc.scalar.dma_start(out=scale[:], in_=docs_scale.rearrange("o k -> (o k)").partition_broadcast(P))
+        nc.scalar.dma_start(out=bias_raw[0][:], in_=c.rearrange("(g p t) -> p g t", g=2, t=4))
+        nc.scalar.dma_start(out=bias_raw[1][:], in_=b.rearrange("(g p t) -> p g t", g=2, t=4))
+        for key in LOADS:
+            if key[0] == "w":
+                h, g = int(key[1]), int(key[2])
+                nc.sync.dma_start(out=x_w[h][g][:], in_=w_v[h, g])
+            if key[0] == "q":
+                h = int(key[1])
+                nc.sync.dma_start(out=x_q[h][:], in_=q_v[h])
+            if key[0] in "dt":
+                dst, src = (x_docs, docs_v) if key[0] == "d" else (x_terms, terms_v)
+                i = int(key[1])
+                cols = slice(0, 4 * D)
+                if len(key) == 3:
+                    cols = slice(int(key[2]) * 2 * D, (int(key[2]) + 1) * 2 * D)
+                nc.sync.dma_start(out=dst[i][:, cols], in_=src[i][:, cols])
+
+        nc.gpsimd.memset(warm[:], 0.0)
+        make_identity(nc, ident[:])
+        nc.scalar.activation(out=warm[:, 1:2], in_=warm[:, 0:1], func=ACT.Relu)
+        for s in range(2):
+            nc.gpsimd.tensor_copy(out=bias[:, s], in_=bias_raw[s][:])
+        nc.scalar.copy(out=scale2[:, 0], in_=scale[:])
+        nc.scalar.copy(out=scale2[:, 1], in_=scale[:])
+
+        def product(i, h):
+            n = D if i == 0 else 2 * D
+            for lo in range(h * 2 * D, (h + 1) * 2 * D, n):
+                nc.vector.tensor_tensor(
+                    out=v_docs[i][:, lo : lo + n],
+                    in0=x_docs[i][:, lo : lo + n].bitcast(FP8),
+                    in1=scale[:] if i == 0 else scale2[:].rearrange("p s k -> p (s k)"),
+                    op=ALU.mult,
+                )
+
+        def turn(words, pair):
+            x = bank()
+            for s in range(2):
+                base = (2 * pair + s) * 256
+                for u in range(2):
+                    k = (2 * s + u) * P
+                    nc.tensor.transpose(x[:, k : k + P], words[:, base + u : base + 256 : 2], ident[:])
+            return x
+
+        def copy(engine, out_ap, in_ap):
+            if engine == "s":
+                nc.scalar.copy(out=out_ap, in_=in_ap)
+            else:
+                nc.vector.tensor_copy(out=out_ap, in_=in_ap)
+
+        def turn_rows(src, dst, pair, engine="s"):
+            x = turn(src.bitcast(F32), pair)
+            copy(
+                engine,
+                dst[:, pair * 256 : (pair + 1) * 256].rearrange("p (s m) t -> p s (m t)", s=2).bitcast(F32).rearrange("p s (m u) -> p s m u", u=2),
+                x[:].rearrange("p (s u m) -> p s m u", s=2, u=2),
+            )
+
+        def turn_docs(i, pair, engine="s"):
+            x = turn(v_docs[i][:].bitcast(F32), pair)
+            dst = g_docs[i][:].rearrange("p n t -> p (n t)").bitcast(F32).rearrange("p (m s u) -> p m s u", s=4, u=2)
+            copy(
+                engine,
+                dst[:, :, 2 * pair : 2 * pair + 2, :],
+                x[:].rearrange("p (s u m) -> p m s u", s=2, u=2),
+            )
+
+        def quantize(dst, src):
+            nc.vector.quantize_mx(out=dst[0][:].bitcast(FP8X4), scales=dst[1][:], in_=src)
+
+        def flat(x):
+            return x[:].rearrange("p n t -> p (n t)")
+
+        def mx(acc, left, m0, right, start, stop, n0=0, n=W):
+            nc.tensor.matmul_mx(
+                out=acc,
+                lhsT=left[0][:, m0 : m0 + P].bitcast(FP8X4),
+                lhsT_scale=left[1][:, m0 : m0 + P],
+                rhs=right[0][:, n0 : n0 + n].bitcast(FP8X4),
+                rhs_scale=right[1][:, n0 : n0 + n],
+                start=start,
+                stop=stop,
+            )
+
+        def w_group(h, g, engine="v"):
+            copy(
+                engine,
+                g_w[h][g][:].rearrange("p (t m j) -> p t m j", t=4, j=4),
+                x_w[h][g][:].rearrange("p j (m t) -> p t m j", t=4),
+            )
+
+        planes = {}
+
+        def match(i, g, engines="ssss"):
+            pl = ring.tile([P, 4, W], BF16, name="planes", bufs=PL)
+            planes[i, g] = pl
+            for t in range(4):
+                acc = bank()
+                mx(acc[:], q_terms[g], t * P, q_docs[i], True, True)
+                col = bias[:, 0, g, t : t + 1]
+                if engines[t] == "s":
+                    nc.scalar.activation(out=pl[:, t], in_=acc[:], func=ACT.Relu, bias=col)
+                else:
+                    nc.vector.tensor_scalar(out=pl[:, t], in0=acc[:], scalar1=col, scalar2=0.0, op0=ALU.add, op1=ALU.max)
+
+        def rewrite(g, engines="ssss"):
+            pl = ring.tile([P, 4, W], BF16, name="planes", bufs=PL)
+            planes["r", g] = pl
+            for t in range(4):
+                acc = bank()
+                for h in range(2):
+                    mx(acc[:], q_w[h][g], t * P, q_q[h], h == 0, h == 1)
+                col = bias[:, 1, g, t : t + 1]
+                if engines[t] == "s":
+                    nc.scalar.activation(out=pl[:, t], in_=acc[:], func=ACT.Identity, bias=col)
+                else:
+                    nc.vector.tensor_scalar(out=pl[:, t], in0=acc[:], scalar1=col, scalar2=None, op0=ALU.add)
+
+        grouped = {}
+
+        def group(key, lo, hi):
+            if key not in grouped:
+                grouped[key] = ring.tile([P, W, 4], BF16, name="grouped", align_bytes=64, bufs=5)
+            nc.vector.tensor_copy(
+                out=grouped[key][:, lo:hi].rearrange("p (c i) t -> p c t i", i=4),
+                in_=planes[key][:, :, lo:hi].rearrange("p t (c i) -> p c t i", i=4),
+            )
+
+        def quantize_m(i, g, lo, hi):
+            nc.vector.quantize_mx(
+                out=q_m[i][g][0][:, lo:hi].bitcast(FP8X4),
+                scales=q_m[i][g][1][:, lo:hi],
+                in_=grouped[i, g][:, lo:hi].rearrange("p n t -> p (n t)"),
+            )
+
+        def quantize_r(g):
+            quantize(q_r[g], flat(grouped["r", g]))
+
+        def score(i, lo, hi, engines="ssss"):
+            accs = [bank() for r in range(4)]
+            for g in range(2):
+                for r in range(4):
+                    mx(accs[r][:, : hi - lo], q_r[g], r * P, q_m[i][g], g == 0, g == 1, lo, hi - lo)
+            for r in range(4):
+                res = ring.tile([P, W], F32, name="res", bufs=10)
+                copy(engines[r], res[:, : hi - lo], accs[r][:, : hi - lo])
+                nc.sync.dma_start(out=out_v[r][:, i * W + lo : i * W + hi], in_=res[:, : hi - lo])
+
+        for step in ORDER:
+            k, e = (step + ":").split(":")[:2]
+            n = [int(x) for x in k[2:]]
+            k = k[:2]
+            if k == "P_":
+                product(n[0], n[1])
+            if k == "Tt":
+                turn_rows(x_terms[n[0]][:], g_terms[n[0]], n[1], e)
+            if k == "Tq":
+                turn_rows(x_q[n[0]][:].rearrange("p r k -> p (r k)"), g_q[n[0]], n[1], e)
+            if k == "Td":
+                turn_docs(n[0], n[1], e)
+            if k == "Qt":
+                quantize(q_terms[n[0]], flat(g_terms[n[0]]))
+            if k == "Qd":
+                quantize(q_docs[n[0]], flat(g_docs[n[0]]))
+            if k == "Qq":
+                quantize(q_q[n[0]], flat(g_q[n[0]]))
+            if k == "Iw":
+                w_group(n[0], n[1], e)
+            if k == "Qw":
+                quantize(q_w[n[0]][n[1]], g_w[n[0]][n[1]][:])
+            if k == "M_":
+                match(n[0], n[1], e)
+            if k == "R_":
+                rewrite(n[0], e)
+            if k == "Gm":
+                group((n[0], n[1]), 0, W)
+            if k == "Gh":
+                group((n[0], n[1]), n[2] * 256, n[2] * 256 + 256)
+            if k == "Gr":
+                group(("r", n[0]), 0, W)
+            if k == "Qm":
+                quantize_m(n[0], n[1], 0, W)
+            if k == "Qh":
+                quantize_m(n[0], n[1], n[2] * 256, n[2] * 256 + 256)
+            if k == "Qr":
+                quantize_r(n[0])
+            if k == "S_":
+                score(n[0], 0, W, e)
+            if k == "Sh":
+                score(n[0], n[1] * 256, n[1] * 256 + 256, e)

@@ -16,21 +16,22 @@ ACT = mybir.ActivationFunctionType
 ALU = mybir.AluOpType
 
 LOADS = [
-    "d00", "d01", "q0", "d1", "d2", "w10", "t1", "t00", "w11", "q1",
-    "w00", "t01", "w01", "d3",
+    "w00", "q0", "d0", "w10", "d3", "d1", "t1", "t0", "q1", "d2",
+    "w11", "w01",
 ]
 ORDER = [
-    "P_00", "Tq00:s", "Td00:s", "Tq01:s", "P_01", "P_10", "P_11",
-    "Iw10:s", "Tt00:s", "P_20", "Tt10:s", "P_21", "Td11:s", "Td01:s",
-    "Qq0", "Iw11:v", "Qd0", "Tq10:s", "Iw00:v", "Tt11:s", "Td10:s",
-    "Td21:s", "Tq11:s", "Tt01:s", "Qt1", "Td20:s", "Iw01:v", "Qt0",
-    "Qq1", "M_01:ssss", "M_00:ssss", "Qw10", "Qw01", "Qw00", "R_0:ssss",
-    "P_30", "Qd1", "Qw11", "Gm00", "Qd2", "Td30:v", "Gm01", "P_31",
-    "R_1:ssss", "Gr1", "M_10:ssss", "Gr0", "Td31:s", "M_11:ssvs",
-    "Qm00", "Qm01", "M_20:ssss", "Qd3", "Qr1", "Qr0", "Gm10", "M_21:ssss",
-    "Gm20", "Qm10", "S_0:svss", "Gm11", "Gm21", "Qm11", "Qm20", "M_31:ssss",
-    "M_30:svss", "Qm21", "Gm30", "Gh311", "S_1:ssss", "Qm30", "S_2:ssss",
-    "Qh311", "Sh31:ssss", "Gh310", "Qh310", "Sh30:svss",
+    "Zz32", "Zs", "Zz04", "Iw00:v", "Tq00:s", "Tq01:s", "Iw10:s",
+    "P_00", "Zz42", "Zz62", "Td00:s", "P_01", "Zb", "Td01:s", "Zz22",
+    "P_30", "P_11", "P_10", "Td30:s", "Tt00:s", "Qd0", "Tt11:s", "Qw00",
+    "Tt10:s", "P_20", "Tq11:s", "Zz72", "Qt1", "P_21", "Td10:s", "Iw11:v",
+    "Tq10:s", "Tt01:s", "Qt0", "M_01:ssss", "Qq0", "Qq1", "Iw01:v",
+    "Qw10", "Td21:s", "M_00:ssss", "Td11:s", "Qw11", "P_31", "Qw01",
+    "Gm00", "Td20:s", "R_0:ssss", "Qd2", "Gr0", "Qd1", "R_1:ssss",
+    "Td31:s", "M_20:svss", "Gm01", "Qm00", "Qd3", "Qm01", "Qr0", "Gr1",
+    "M_10:ssss", "M_21:sssv", "Gm20", "M_31:svss", "M_11:sssv", "M_30:ssss",
+    "Zz52", "Qr1", "Gm10", "Gm11", "S_0:ssss", "Qm10", "Qm11", "Gm21",
+    "Qm20", "Qm21", "Gm30", "Gh310", "S_1:ssss", "S_2:ssss", "Qm30",
+    "Qh310", "Sh30:ssss", "Gh311", "Qh311", "Sh31:svss",
 ]
 PL = 5
 
@@ -58,10 +59,14 @@ def tile_query_rewrite_scoring_s7_kernel(
             )
 
         ident = keep.tile([P, P], F32, name="ident")
-        bias_raw = [keep.tile([P, 2, 4], BF16, name=f"bias_raw{s}") for s in range(2)]
-        bias = keep.tile([P, 2, 2, 4], F32, name="bias")
+        perm = keep.tile([P, P], F32, name="perm")
+        ident_bf = keep.tile([P, P], BF16, name="ident_bf")
+        ones = keep.tile([P, P], F32, name="ones")
+        zeros = keep.tile([P, W], BF16, name="zeros")
+        bias_rows = keep.tile([P, P], BF16, name="bias_rows")
+        bias = keep.tile([P, 16], F32, name="bias")
         warm = keep.tile([P, 2], F32, name="warm")
-        scale = keep.tile([P, D], F32, name="scale")
+        scale_row = keep.tile([P, D], F32, name="scale_row")
         scale2 = keep.tile([P, 2, D], F32, name="scale2")
         x_docs = [keep.tile([P, 4 * D], U8, name=f"x_docs{i}") for i in range(4)]
         v_docs = [keep.tile([P, 4 * D], BF16, name=f"v_docs{i}") for i in range(4)]
@@ -83,11 +88,17 @@ def tile_query_rewrite_scoring_s7_kernel(
         terms_v = terms.rearrange("(g m j) k -> g m (j k)", g=2, j=4)
         q_v = queries.rearrange("(m r) (h k) -> h m r k", r=4, h=2)
         w_v = w.rearrange("(h p j) (g c) -> h g p j c", h=2, j=4, g=2)
-        out_v = out.rearrange("(m r) n -> r m n", r=4)
+        out_v = out.rearrange("(r m) n -> r m n", r=4)
 
-        nc.scalar.dma_start(out=scale[:], in_=docs_scale.rearrange("o k -> (o k)").partition_broadcast(P))
-        nc.scalar.dma_start(out=bias_raw[0][:], in_=c.rearrange("(g p t) -> p g t", g=2, t=4))
-        nc.scalar.dma_start(out=bias_raw[1][:], in_=b.rearrange("(g p t) -> p g t", g=2, t=4))
+        nc.gpsimd.memset(scale_row[:], 0.0)
+        nc.vector.memset(bias_rows[:], 0.0)
+        nc.vector.memset(zeros[:], 0.0)
+        nc.scalar.dma_start(out=scale_row[0:1, :], in_=docs_scale)
+        for s, vec in enumerate((c, b)):
+            src = vec.rearrange("(g a j q) -> g j a q", g=2, a=16, j=4)
+            for g in range(2):
+                row = 8 * s + 4 * g
+                nc.scalar.dma_start(out=bias_rows[row : row + 4, :].rearrange("j (a q) -> j a q", a=16), in_=src[g])
         for key in LOADS:
             if key[0] == "w":
                 h, g = int(key[1]), int(key[2])
@@ -103,31 +114,46 @@ def tile_query_rewrite_scoring_s7_kernel(
                     cols = slice(int(key[2]) * 2 * D, (int(key[2]) + 1) * 2 * D)
                 nc.sync.dma_start(out=dst[i][:, cols], in_=src[i][:, cols])
 
+        nc.gpsimd.memset(ones[:], 1.0)
         nc.gpsimd.memset(warm[:], 0.0)
         make_identity(nc, ident[:])
         nc.scalar.activation(out=warm[:, 1:2], in_=warm[:, 0:1], func=ACT.Relu)
-        for s in range(2):
-            nc.gpsimd.tensor_copy(out=bias[:, s], in_=bias_raw[s][:])
-        nc.scalar.copy(out=scale2[:, 0], in_=scale[:])
-        nc.scalar.copy(out=scale2[:, 1], in_=scale[:])
+        nc.vector.tensor_copy(out=perm[:].rearrange("p (j a h) -> p j a h", j=4, a=16), in_=ident[:].rearrange("p (a j h) -> p j a h", j=4, a=16))
+        nc.vector.tensor_copy(out=ident_bf[:], in_=ident[:])
+
+        def spread_scale():
+            x = bank()
+            nc.tensor.matmul(x[:], ones[:], scale_row[:], start=True, stop=True)
+            for s in range(2):
+                nc.scalar.copy(out=scale2[:, s], in_=x[:])
+
+        def spread_bias():
+            x = bank()
+            turned = x[:].bitcast(BF16)
+            nc.tensor.transpose(turned[:, :P], bias_rows[:], ident_bf[:])
+            nc.scalar.copy(out=bias[:], in_=turned[:, :16])
+
+        def keep_warm(n):
+            x = bank()
+            for s in range(n):
+                nc.tensor.matmul(x[:], zeros[:, :P], zeros[:], start=True, stop=True)
 
         def product(i, h):
-            n = D if i == 0 else 2 * D
-            for lo in range(h * 2 * D, (h + 1) * 2 * D, n):
-                nc.vector.tensor_tensor(
-                    out=v_docs[i][:, lo : lo + n],
-                    in0=x_docs[i][:, lo : lo + n].bitcast(FP8),
-                    in1=scale[:] if i == 0 else scale2[:].rearrange("p s k -> p (s k)"),
-                    op=ALU.mult,
-                )
+            cols = slice(h * 2 * D, (h + 1) * 2 * D)
+            nc.vector.tensor_tensor(
+                out=v_docs[i][:, cols],
+                in0=x_docs[i][:, cols].bitcast(FP8),
+                in1=scale2[:].rearrange("p s k -> p (s k)"),
+                op=ALU.mult,
+            )
 
-        def turn(words, pair):
+        def turn(words, pair, order):
             x = bank()
             for s in range(2):
                 base = (2 * pair + s) * 256
                 for u in range(2):
                     k = (2 * s + u) * P
-                    nc.tensor.transpose(x[:, k : k + P], words[:, base + u : base + 256 : 2], ident[:])
+                    nc.tensor.transpose(x[:, k : k + P], words[:, base + u : base + 256 : 2], order[:])
             return x
 
         def copy(engine, out_ap, in_ap):
@@ -136,22 +162,10 @@ def tile_query_rewrite_scoring_s7_kernel(
             else:
                 nc.vector.tensor_copy(out=out_ap, in_=in_ap)
 
-        def turn_rows(src, dst, pair, engine="s"):
-            x = turn(src.bitcast(F32), pair)
-            copy(
-                engine,
-                dst[:, pair * 256 : (pair + 1) * 256].rearrange("p (s m) t -> p s (m t)", s=2).bitcast(F32).rearrange("p s (m u) -> p s m u", u=2),
-                x[:].rearrange("p (s u m) -> p s m u", s=2, u=2),
-            )
-
-        def turn_docs(i, pair, engine="s"):
-            x = turn(v_docs[i][:].bitcast(F32), pair)
-            dst = g_docs[i][:].rearrange("p n t -> p (n t)").bitcast(F32).rearrange("p (m s u) -> p m s u", s=4, u=2)
-            copy(
-                engine,
-                dst[:, :, 2 * pair : 2 * pair + 2, :],
-                x[:].rearrange("p (s u m) -> p m s u", s=2, u=2),
-            )
+        def turn_rows(src, dst, pair, engine="s", order=ident):
+            x = turn(src.bitcast(F32), pair, order)
+            view = dst[:].rearrange("p n t -> p (n t)").bitcast(F32).rearrange("p (m v) -> p m v", v=8)
+            copy(engine, view[:, :, 4 * pair : 4 * pair + 4], x[:].rearrange("p (v m) -> p m v", v=4))
 
         def quantize(dst, src):
             nc.vector.quantize_mx(out=dst[0][:].bitcast(FP8X4), scales=dst[1][:], in_=src)
@@ -173,8 +187,8 @@ def tile_query_rewrite_scoring_s7_kernel(
         def w_group(h, g, engine="v"):
             copy(
                 engine,
-                g_w[h][g][:].rearrange("p (t m j) -> p t m j", t=4, j=4),
-                x_w[h][g][:].rearrange("p j (m t) -> p t m j", t=4),
+                g_w[h][g][:].rearrange("p (t a q j) -> p t a q j", t=4, a=16, j=4),
+                x_w[h][g][:].rearrange("p j (a t q) -> p t a q j", t=4, a=16),
             )
 
         planes = {}
@@ -185,7 +199,7 @@ def tile_query_rewrite_scoring_s7_kernel(
             for t in range(4):
                 acc = bank()
                 mx(acc[:], q_terms[g], t * P, q_docs[i], True, True)
-                col = bias[:, 0, g, t : t + 1]
+                col = bias[:, 4 * g + t : 4 * g + t + 1]
                 if engines[t] == "s":
                     nc.scalar.activation(out=pl[:, t], in_=acc[:], func=ACT.Relu, bias=col)
                 else:
@@ -198,7 +212,7 @@ def tile_query_rewrite_scoring_s7_kernel(
                 acc = bank()
                 for h in range(2):
                     mx(acc[:], q_w[h][g], t * P, q_q[h], h == 0, h == 1)
-                col = bias[:, 1, g, t : t + 1]
+                col = bias[:, 8 + 4 * g + t : 8 + 4 * g + t + 1]
                 if engines[t] == "s":
                     nc.scalar.activation(out=pl[:, t], in_=acc[:], func=ACT.Identity, bias=col)
                 else:
@@ -238,14 +252,20 @@ def tile_query_rewrite_scoring_s7_kernel(
             k, e = (step + ":").split(":")[:2]
             n = [int(x) for x in k[2:]]
             k = k[:2]
+            if k == "Zs":
+                spread_scale()
+            if k == "Zb":
+                spread_bias()
+            if k == "Zz":
+                keep_warm(n[1])
             if k == "P_":
                 product(n[0], n[1])
             if k == "Tt":
-                turn_rows(x_terms[n[0]][:], g_terms[n[0]], n[1], e)
+                turn_rows(x_terms[n[0]][:], g_terms[n[0]], n[1], e, perm)
             if k == "Tq":
                 turn_rows(x_q[n[0]][:].rearrange("p r k -> p (r k)"), g_q[n[0]], n[1], e)
             if k == "Td":
-                turn_docs(n[0], n[1], e)
+                turn_rows(v_docs[n[0]][:], g_docs[n[0]], n[1], e)
             if k == "Qt":
                 quantize(q_terms[n[0]], flat(g_terms[n[0]]))
             if k == "Qd":

@@ -16,22 +16,22 @@ ACT = mybir.ActivationFunctionType
 ALU = mybir.AluOpType
 
 LOADS = [
-    "w00", "q0", "d0", "w10", "d3", "d1", "t1", "t0", "q1", "d2",
-    "w11", "w01",
+    "s", "w10", "t1", "d1", "w000", "t00", "d0", "t01", "w001", "w01",
+    "d2", "b", "d3", "w11", "q1", "q0",
 ]
 ORDER = [
-    "Zz32", "Zs", "Zz04", "Iw00:v", "Tq00:s", "Tq01:s", "Iw10:s",
-    "P_00", "Zz42", "Zz62", "Td00:s", "P_01", "Zb", "Td01:s", "Zz22",
-    "P_30", "P_11", "P_10", "Td30:s", "Tt00:s", "Qd0", "Tt11:s", "Qw00",
-    "Tt10:s", "P_20", "Tq11:s", "Zz72", "Qt1", "P_21", "Td10:s", "Iw11:v",
-    "Tq10:s", "Tt01:s", "Qt0", "M_01:ssss", "Qq0", "Qq1", "Iw01:v",
-    "Qw10", "Td21:s", "M_00:ssss", "Td11:s", "Qw11", "P_31", "Qw01",
-    "Gm00", "Td20:s", "R_0:ssss", "Qd2", "Gr0", "Qd1", "R_1:ssss",
-    "Td31:s", "M_20:svss", "Gm01", "Qm00", "Qd3", "Qm01", "Qr0", "Gr1",
-    "M_10:ssss", "M_21:sssv", "Gm20", "M_31:svss", "M_11:sssv", "M_30:ssss",
-    "Zz52", "Qr1", "Gm10", "Gm11", "S_0:ssss", "Qm10", "Qm11", "Gm21",
-    "Qm20", "Qm21", "Gm30", "Gh310", "S_1:ssss", "S_2:ssss", "Qm30",
-    "Qh310", "Sh30:ssss", "Gh311", "Qh311", "Sh31:svss",
+    "Iw10:v", "Zs", "Tt10:s", "Qw10", "Iv000:s", "Zz1:2", "P_11",
+    "Tt11:s", "P_10", "Tt00:s", "P_01", "Qt1", "Zz3:0", "Td11:s",
+    "P_00", "Tt01:s", "Td10:s", "Zz2:2", "Qd1", "P_20", "Iv001:s",
+    "Qt0", "Jw01:ss", "P_21", "Td01:s", "Zb", "Zz0:0", "Td00:s", "P_31",
+    "Qd0", "P_30", "M_10:ssss", "Zz6:0", "Tq10:s", "Td20:v", "M_11:svsv",
+    "Qw01", "Gm10", "Tq00:s", "Tq01:s", "Qq0", "Qw00", "M_01:ssss",
+    "Jw11:ss", "Gm11", "Gm01", "Td21:s", "Qd2", "Td30:s", "Td31:s",
+    "Qd3", "Tq11:s", "Qq1", "M_00:ssss", "Qm10", "M_21:ssss", "Qm11",
+    "Rn0", "Qw11", "Gm00", "M_31:ssss", "Zz4:0", "Qr0", "M_20:ssss",
+    "Rn1", "Qm01", "M_30:ssss", "Qr1", "Qm00", "S_1:ssss", "Gm20",
+    "Gm21", "Qm20", "Qm21", "Zz5:0", "Gm30", "Gh311", "S_0:ssss",
+    "Qm30", "S_2:ssss", "Qh311", "Gh310", "Sh31:svss", "Qh310", "Sh30:svvv",
 ]
 PL = 5
 
@@ -91,18 +91,23 @@ def tile_query_rewrite_scoring_s7_kernel(
         out_v = out.rearrange("(r m) n -> r m n", r=4)
 
         nc.gpsimd.memset(scale_row[:], 0.0)
-        nc.vector.memset(bias_rows[:], 0.0)
         nc.vector.memset(zeros[:], 0.0)
-        nc.scalar.dma_start(out=scale_row[0:1, :], in_=docs_scale)
-        for s, vec in enumerate((c, b)):
-            src = vec.rearrange("(g a j q) -> g j a q", g=2, a=16, j=4)
-            for g in range(2):
-                row = 8 * s + 4 * g
-                nc.scalar.dma_start(out=bias_rows[row : row + 4, :].rearrange("j (a q) -> j a q", a=16), in_=src[g])
+        nc.vector.memset(bias_rows[:], 0.0)
         for key in LOADS:
+            if key == "s":
+                nc.sync.dma_start(out=scale_row[0:1, :], in_=docs_scale)
+            if key == "b":
+                for s, vec in enumerate((c, b)):
+                    src = vec.rearrange("(g a j q) -> g j a q", g=2, a=16, j=4)
+                    for g in range(2):
+                        row = 8 * s + 4 * g
+                        nc.sync.dma_start(out=bias_rows[row : row + 4, :].rearrange("j (a q) -> j a q", a=16), in_=src[g])
             if key[0] == "w":
                 h, g = int(key[1]), int(key[2])
-                nc.sync.dma_start(out=x_w[h][g][:], in_=w_v[h, g])
+                cols = slice(0, W)
+                if len(key) == 4:
+                    cols = slice(int(key[3]) * 256, int(key[3]) * 256 + 256)
+                nc.sync.dma_start(out=x_w[h][g][:, :, cols], in_=w_v[h, g][:, :, cols])
             if key[0] == "q":
                 h = int(key[1])
                 nc.sync.dma_start(out=x_q[h][:], in_=q_v[h])
@@ -134,6 +139,8 @@ def tile_query_rewrite_scoring_s7_kernel(
             nc.scalar.copy(out=bias[:], in_=turned[:, :16])
 
         def keep_warm(n):
+            if n == 0:
+                return
             x = bank()
             for s in range(n):
                 nc.tensor.matmul(x[:], zeros[:, :P], zeros[:], start=True, stop=True)
@@ -191,6 +198,27 @@ def tile_query_rewrite_scoring_s7_kernel(
                 x_w[h][g][:].rearrange("p j (a t q) -> p t a q j", t=4, a=16),
             )
 
+        def w_group_half(h, g, half, engine):
+            lo = half * 256
+            copy(
+                engine,
+                g_w[h][g][:].rearrange("p (t a q j) -> p t a (q j)", t=4, a=16, j=4)[:, :, half * 8 : half * 8 + 8].rearrange("p t a (q j) -> p t a q j", j=4),
+                x_w[h][g][:, :, lo : lo + 256].rearrange("p j (a t q) -> p t a q j", t=4, a=8),
+            )
+
+        def w_group_pe(h, g, engines):
+            for half in range(2):
+                x = psum.tile([P, 2 * W], BF16, name="bank")
+                for s in range(2):
+                    nc.tensor.matmul(
+                        x[:, s * W : (s + 1) * W].rearrange("p (a q j) -> p a q j", a=16, j=4),
+                        ident_bf[:],
+                        x_w[h][g][:].rearrange("p j (a t q) -> p t a q j", t=4, a=16)[:, 2 * half + s],
+                        start=True,
+                        stop=True,
+                    )
+                copy(engines[half], g_w[h][g][:, half * 2 * W : (half + 1) * 2 * W], x[:])
+
         planes = {}
 
         def match(i, g, engines="ssss"):
@@ -235,6 +263,22 @@ def tile_query_rewrite_scoring_s7_kernel(
                 in_=grouped[i, g][:, lo:hi].rearrange("p n t -> p (n t)"),
             )
 
+        def rewrite_direct(g):
+            gr = ring.tile([P, W, 4], BF16, name="grouped", align_bytes=64, bufs=5)
+            grouped["r", g] = gr
+            shift = bias[:, 8 + 4 * g : 12 + 4 * g].unsqueeze(1).to_broadcast([P, P, 4])
+            for r in range(4):
+                acc = bank()
+                for t in range(4):
+                    for h in range(2):
+                        mx(acc[:, t * P : (t + 1) * P], q_w[h][g], t * P, q_q[h], h == 0, h == 1, r * P, P)
+                nc.vector.tensor_tensor(
+                    out=gr[:, r * P : (r + 1) * P],
+                    in0=acc[:].rearrange("p (t n) -> p n t", t=4),
+                    in1=shift,
+                    op=ALU.add,
+                )
+
         def quantize_r(g):
             quantize(q_r[g], flat(grouped["r", g]))
 
@@ -250,14 +294,14 @@ def tile_query_rewrite_scoring_s7_kernel(
 
         for step in ORDER:
             k, e = (step + ":").split(":")[:2]
-            n = [int(x) for x in k[2:]]
+            n = [int(x) for x in k[2:] if k[1] != 'z']
             k = k[:2]
             if k == "Zs":
                 spread_scale()
             if k == "Zb":
                 spread_bias()
             if k == "Zz":
-                keep_warm(n[1])
+                keep_warm(int(e))
             if k == "P_":
                 product(n[0], n[1])
             if k == "Tt":
@@ -274,12 +318,18 @@ def tile_query_rewrite_scoring_s7_kernel(
                 quantize(q_q[n[0]], flat(g_q[n[0]]))
             if k == "Iw":
                 w_group(n[0], n[1], e)
+            if k == "Iv":
+                w_group_half(n[0], n[1], n[2], e)
+            if k == "Jw":
+                w_group_pe(n[0], n[1], e)
             if k == "Qw":
                 quantize(q_w[n[0]][n[1]], g_w[n[0]][n[1]][:])
             if k == "M_":
                 match(n[0], n[1], e)
             if k == "R_":
                 rewrite(n[0], e)
+            if k == "Rn":
+                rewrite_direct(n[0])
             if k == "Gm":
                 group((n[0], n[1]), 0, W)
             if k == "Gh":

@@ -16,22 +16,22 @@ ACT = mybir.ActivationFunctionType
 ALU = mybir.AluOpType
 
 LOADS = [
-    "s", "w10", "t1", "d1", "w000", "t00", "d0", "t01", "w001", "w01",
-    "d2", "b", "d3", "w11", "q1", "q0",
+    "s", "t00", "d2", "t01", "w001", "t1", "d1", "w11", "w000", "d0",
+    "w01", "b", "q1", "d3", "q0", "w10",
 ]
 ORDER = [
-    "Iw10:v", "Zs", "Tt10:s", "Qw10", "Iv000:s", "Zz1:2", "P_11",
-    "Tt11:s", "P_10", "Tt00:s", "P_01", "Qt1", "Zz3:0", "Td11:s",
-    "P_00", "Tt01:s", "Td10:s", "Zz2:2", "Qd1", "P_20", "Iv001:s",
-    "Qt0", "Jw01:ss", "P_21", "Td01:s", "Zb", "Zz0:0", "Td00:s", "P_31",
-    "Qd0", "P_30", "M_10:ssss", "Zz6:0", "Tq10:s", "Td20:v", "M_11:svsv",
-    "Qw01", "Gm10", "Tq00:s", "Tq01:s", "Qq0", "Qw00", "M_01:ssss",
-    "Jw11:ss", "Gm11", "Gm01", "Td21:s", "Qd2", "Td30:s", "Td31:s",
-    "Qd3", "Tq11:s", "Qq1", "M_00:ssss", "Qm10", "M_21:ssss", "Qm11",
-    "Rn0", "Qw11", "Gm00", "M_31:ssss", "Zz4:0", "Qr0", "M_20:ssss",
-    "Rn1", "Qm01", "M_30:ssss", "Qr1", "Qm00", "S_1:ssss", "Gm20",
-    "Gm21", "Qm20", "Qm21", "Zz5:0", "Gm30", "Gh311", "S_0:ssss",
-    "Qm30", "S_2:ssss", "Qh311", "Gh310", "Sh31:svss", "Qh310", "Sh30:svvv",
+    "Zz6:3", "Zz3:1", "Zs", "P_21", "P_20", "Tt00:s", "Zz2:2", "Iv001:s",
+    "Tt01:s", "Td21:s", "Tt11:s", "P_10", "Tt10:s", "P_11", "Qt1",
+    "P_00", "Iv000:s", "P_01", "Zz0:2", "Jw11:ss", "Td11:s", "Qw00",
+    "Qt0", "Td20:s", "Td10:s", "Jw01:ss", "Tq11:s", "Zb", "Zz4:0",
+    "Qd1", "P_31", "Td00:s", "M_10:ssss", "Qd2", "Td01:s", "Tq00:s",
+    "Qw01", "Qw11", "P_30", "Gm10", "Tq01:s", "Qd0", "M_21:ssss",
+    "Mn11", "Tq10:s", "Jw10:ss", "Td31:s", "Td30:s", "Qq0", "Gm21",
+    "M_01:ssss", "Me11", "Qw10", "Qq1", "Qm10", "M_20:ssss", "Qd3",
+    "Rn0", "Gm20", "Qm11", "Qr0", "M_00:ssss", "M_31:ssss", "Rn1",
+    "Qm21", "Qr1", "M_30:ssss", "S_1:ssss", "Qm20", "Gm00", "Gm01",
+    "Qm00", "S_2:ssss", "Qm01", "S_0:ssss", "Zz5:0", "Gm30", "Gh310",
+    "Qm30", "Qh310", "Zz1:0", "Gh311", "Sh30:svss", "Qh311", "Sh31:ssss",
 ]
 PL = 5
 
@@ -62,12 +62,12 @@ def tile_query_rewrite_scoring_s7_kernel(
         perm = keep.tile([P, P], F32, name="perm")
         ident_bf = keep.tile([P, P], BF16, name="ident_bf")
         ones = keep.tile([P, P], F32, name="ones")
-        zeros = keep.tile([P, W], BF16, name="zeros")
+        zeros = keep.tile([P, W // 2], F32, name="zeros")
         bias_rows = keep.tile([P, P], BF16, name="bias_rows")
         bias = keep.tile([P, 16], F32, name="bias")
         warm = keep.tile([P, 2], F32, name="warm")
         scale_row = keep.tile([P, D], F32, name="scale_row")
-        scale2 = keep.tile([P, 2, D], F32, name="scale2")
+        scale = keep.tile([P, D], F32, name="scale")
         x_docs = [keep.tile([P, 4 * D], U8, name=f"x_docs{i}") for i in range(4)]
         v_docs = [keep.tile([P, 4 * D], BF16, name=f"v_docs{i}") for i in range(4)]
         x_terms = [keep.tile([P, 4 * D], BF16, name=f"x_terms{g}") for g in range(2)]
@@ -90,8 +90,8 @@ def tile_query_rewrite_scoring_s7_kernel(
         w_v = w.rearrange("(h p j) (g c) -> h g p j c", h=2, j=4, g=2)
         out_v = out.rearrange("(r m) n -> r m n", r=4)
 
+        nc.gpsimd.memset(zeros[:], 0.0)
         nc.gpsimd.memset(scale_row[:], 0.0)
-        nc.vector.memset(zeros[:], 0.0)
         nc.vector.memset(bias_rows[:], 0.0)
         for key in LOADS:
             if key == "s":
@@ -129,8 +129,7 @@ def tile_query_rewrite_scoring_s7_kernel(
         def spread_scale():
             x = bank()
             nc.tensor.matmul(x[:], ones[:], scale_row[:], start=True, stop=True)
-            for s in range(2):
-                nc.scalar.copy(out=scale2[:, s], in_=x[:])
+            nc.scalar.copy(out=scale[:], in_=x[:])
 
         def spread_bias():
             x = bank()
@@ -143,16 +142,14 @@ def tile_query_rewrite_scoring_s7_kernel(
                 return
             x = bank()
             for s in range(n):
-                nc.tensor.matmul(x[:], zeros[:, :P], zeros[:], start=True, stop=True)
+                nc.tensor.matmul(x[:], zeros[:].bitcast(BF16)[:, :P], zeros[:].bitcast(BF16), start=True, stop=True)
 
         def product(i, h):
-            cols = slice(h * 2 * D, (h + 1) * 2 * D)
-            nc.vector.tensor_tensor(
-                out=v_docs[i][:, cols],
-                in0=x_docs[i][:, cols].bitcast(FP8),
-                in1=scale2[:].rearrange("p s k -> p (s k)"),
-                op=ALU.mult,
-            )
+            for s in (2 * h, 2 * h + 1):
+                row = slice(s * D, (s + 1) * D)
+                nc.vector.tensor_tensor(
+                    out=v_docs[i][:, row], in0=x_docs[i][:, row].bitcast(FP8), in1=scale[:], op=ALU.mult
+                )
 
         def turn(words, pair, order):
             x = bank()
@@ -248,9 +245,13 @@ def tile_query_rewrite_scoring_s7_kernel(
 
         grouped = {}
 
-        def group(key, lo, hi):
+        def new_group(key):
             if key not in grouped:
                 grouped[key] = ring.tile([P, W, 4], BF16, name="grouped", align_bytes=64, bufs=5)
+            return grouped[key]
+
+        def group(key, lo, hi):
+            new_group(key)
             nc.vector.tensor_copy(
                 out=grouped[key][:, lo:hi].rearrange("p (c i) t -> p c t i", i=4),
                 in_=planes[key][:, :, lo:hi].rearrange("p t (c i) -> p c t i", i=4),
@@ -264,8 +265,7 @@ def tile_query_rewrite_scoring_s7_kernel(
             )
 
         def rewrite_direct(g):
-            gr = ring.tile([P, W, 4], BF16, name="grouped", align_bytes=64, bufs=5)
-            grouped["r", g] = gr
+            gr = new_group(("r", g))
             shift = bias[:, 8 + 4 * g : 12 + 4 * g].unsqueeze(1).to_broadcast([P, P, 4])
             for r in range(4):
                 acc = bank()
@@ -278,6 +278,24 @@ def tile_query_rewrite_scoring_s7_kernel(
                     in1=shift,
                     op=ALU.add,
                 )
+
+        def match_direct(i, g):
+            gr = new_group((i, g))
+            shift = bias[:, 4 * g : 4 * g + 4].unsqueeze(1).to_broadcast([P, P, 4])
+            for n in range(4):
+                acc = bank()
+                for t in range(4):
+                    mx(acc[:, t * P : (t + 1) * P], q_terms[g], t * P, q_docs[i], True, True, n * P, P)
+                nc.vector.tensor_tensor(
+                    out=gr[:, n * P : (n + 1) * P],
+                    in0=acc[:].rearrange("p (t n) -> p n t", t=4),
+                    in1=shift,
+                    op=ALU.add,
+                )
+
+        def rectify(i, g):
+            x = grouped[i, g][:].rearrange("p n t -> p (n t)")
+            nc.vector.tensor_scalar(out=x, in0=x, scalar1=0.0, scalar2=None, op0=ALU.max)
 
         def quantize_r(g):
             quantize(q_r[g], flat(grouped["r", g]))
@@ -328,6 +346,10 @@ def tile_query_rewrite_scoring_s7_kernel(
                 match(n[0], n[1], e)
             if k == "R_":
                 rewrite(n[0], e)
+            if k == "Mn":
+                match_direct(n[0], n[1])
+            if k == "Me":
+                rectify(n[0], n[1])
             if k == "Rn":
                 rewrite_direct(n[0])
             if k == "Gm":

from contextlib import ExitStack

import concourse.mybir as mybir
from concourse.masks import make_identity

B, K, T, D, N = 512, 1024, 1024, 512, 2048
FLOPS = 2 * (B * K * T + T * D * N + B * T * N)

F32 = mybir.dt.float32
BF16 = mybir.dt.bfloat16
U32 = mybir.dt.uint32
U8 = mybir.dt.uint8
FP8 = mybir.dt.float8_e4m3fn
FP8X4 = mybir.dt.float8_e4m3fn_x4
ACT = mybir.ActivationFunctionType
ALU = mybir.AluOpType

LOADS = [
    "s", "t00", "d2", "t01", "w001", "t1", "d1", "w11", "w000", "d0",
    "w01", "b", "q1", "d3", "q0", "w10",
]
ORDER = [
    "Zz6:3", "Zz3:1", "Zs", "P_21", "P_20", "Tt00:s", "Zz2:2", "Iv001:s",
    "Tt01:s", "Td21:s", "Tt11:s", "P_10", "Tt10:s", "P_11", "Qt1",
    "P_00", "Iv000:s", "P_01", "Zz0:2", "Jw11:ss", "Td11:s", "Qw00",
    "Qt0", "Td20:s", "Td10:s", "Jw01:ss", "Tq11:s", "Zb", "Zz4:0",
    "Qd1", "P_31", "Td00:s", "M_10:ssss", "Qd2", "Td01:s", "Tq00:s",
    "Qw01", "Qw11", "P_30", "Gm10", "Tq01:s", "Qd0", "M_21:ssss",
    "Mn11", "Tq10:s", "Jw10:ss", "Td31:s", "Td30:s", "Qq0", "Gm21",
    "M_01:ssss", "Me11", "Qw10", "Qq1", "Qm10", "M_20:ssss", "Qd3",
    "Rn0", "Gm20", "Qm11", "Qr0", "M_00:ssss", "M_31:ssss", "Rn1",
    "Qm21", "Qr1", "M_30:ssss", "S_1:ssss", "Qm20", "Gm00", "Gm01",
    "Qm00", "S_2:ssss", "Qm01", "S_0:ssss", "Zz5:0", "Gm30", "Gh310",
    "Qm30", "Qh310", "Zz1:0", "Gh311", "Sh30:svss", "Qh311", "Sh31:ssss",
]
PL = 5

P = 128
W = 512


def tile_query_rewrite_scoring_s7_kernel(
    tc, queries, w, b, terms, c, docs_bytes, docs_scale, out
):
    nc = tc.nc
    with ExitStack() as ctx:
        keep = ctx.enter_context(tc.tile_pool(name="keep", bufs=1))
        ring = ctx.enter_context(tc.tile_pool(name="ring", bufs=3))
        psum = ctx.enter_context(tc.psum_pool(name="psum", bufs=8))
        ctx.enter_context(tc.manual_schedule())

        def bank():
            return psum.tile([P, W], F32, name="bank")

        def codes(name):
            return (
                keep.tile([P, W], U32, name=name + "_codes", align_bytes=64),
                keep.tile([P, W], U8, name=name + "_scales", align_bytes=64),
            )

        ident = keep.tile([P, P], F32, name="ident")
        perm = keep.tile([P, P], F32, name="perm")
        ident_bf = keep.tile([P, P], BF16, name="ident_bf")
        ones = keep.tile([P, P], F32, name="ones")
        zeros = keep.tile([P, W // 2], F32, name="zeros")
        bias_rows = keep.tile([P, P], BF16, name="bias_rows")
        bias = keep.tile([P, 16], F32, name="bias")
        warm = keep.tile([P, 2], F32, name="warm")
        scale_row = keep.tile([P, D], F32, name="scale_row")
        scale = keep.tile([P, D], F32, name="scale")
        x_docs = [keep.tile([P, 4 * D], U8, name=f"x_docs{i}") for i in range(4)]
        v_docs = [keep.tile([P, 4 * D], BF16, name=f"v_docs{i}") for i in range(4)]
        x_terms = [keep.tile([P, 4 * D], BF16, name=f"x_terms{g}") for g in range(2)]
        x_q = [keep.tile([P, 4, 512], BF16, name=f"x_q{h}") for h in range(2)]
        x_w = [[keep.tile([P, 4, W], BF16, name=f"x_w{h}{g}") for g in range(2)] for h in range(2)]
        g_docs = [keep.tile([P, W, 4], BF16, name=f"g_docs{i}", align_bytes=64) for i in range(4)]
        g_terms = [keep.tile([P, W, 4], BF16, name=f"g_terms{g}", align_bytes=64) for g in range(2)]
        g_q = [keep.tile([P, W, 4], BF16, name=f"g_q{h}", align_bytes=64) for h in range(2)]
        g_w = [[keep.tile([P, W * 4], BF16, name=f"g_w{h}{g}", align_bytes=64) for g in range(2)] for h in range(2)]
        q_docs = [codes(f"q_docs{i}") for i in range(4)]
        q_terms = [codes(f"q_terms{g}") for g in range(2)]
        q_q = [codes(f"q_q{h}") for h in range(2)]
        q_w = [[codes(f"q_w{h}{g}") for g in range(2)] for h in range(2)]
        q_r = [codes(f"q_r{g}") for g in range(2)]
        q_m = [[codes(f"q_m{i}{g}") for g in range(2)] for i in range(4)]

        docs_v = docs_bytes.rearrange("(i m s) k -> i m (s k)", i=4, s=4)
        terms_v = terms.rearrange("(g m j) k -> g m (j k)", g=2, j=4)
        q_v = queries.rearrange("(m r) (h k) -> h m r k", r=4, h=2)
        w_v = w.rearrange("(h p j) (g c) -> h g p j c", h=2, j=4, g=2)
        out_v = out.rearrange("(r m) n -> r m n", r=4)

        nc.gpsimd.memset(zeros[:], 0.0)
        nc.gpsimd.memset(scale_row[:], 0.0)
        nc.vector.memset(bias_rows[:], 0.0)
        for key in LOADS:
            if key == "s":
                nc.sync.dma_start(out=scale_row[0:1, :], in_=docs_scale)
            if key == "b":
                for s, vec in enumerate((c, b)):
                    src = vec.rearrange("(g a j q) -> g j a q", g=2, a=16, j=4)
                    for g in range(2):
                        row = 8 * s + 4 * g
                        nc.sync.dma_start(out=bias_rows[row : row + 4, :].rearrange("j (a q) -> j a q", a=16), in_=src[g])
            if key[0] == "w":
                h, g = int(key[1]), int(key[2])
                cols = slice(0, W)
                if len(key) == 4:
                    cols = slice(int(key[3]) * 256, int(key[3]) * 256 + 256)
                nc.sync.dma_start(out=x_w[h][g][:, :, cols], in_=w_v[h, g][:, :, cols])
            if key[0] == "q":
                h = int(key[1])
                nc.sync.dma_start(out=x_q[h][:], in_=q_v[h])
            if key[0] in "dt":
                dst, src = (x_docs, docs_v) if key[0] == "d" else (x_terms, terms_v)
                i = int(key[1])
                cols = slice(0, 4 * D)
                if len(key) == 3:
                    cols = slice(int(key[2]) * 2 * D, (int(key[2]) + 1) * 2 * D)
                nc.sync.dma_start(out=dst[i][:, cols], in_=src[i][:, cols])

        nc.gpsimd.memset(ones[:], 1.0)
        nc.gpsimd.memset(warm[:], 0.0)
        make_identity(nc, ident[:])
        nc.scalar.activation(out=warm[:, 1:2], in_=warm[:, 0:1], func=ACT.Relu)
        nc.vector.tensor_copy(out=perm[:].rearrange("p (j a h) -> p j a h", j=4, a=16), in_=ident[:].rearrange("p (a j h) -> p j a h", j=4, a=16))
        nc.vector.tensor_copy(out=ident_bf[:], in_=ident[:])

        def spread_scale():
            x = bank()
            nc.tensor.matmul(x[:], ones[:], scale_row[:], start=True, stop=True)
            nc.scalar.copy(out=scale[:], in_=x[:])

        def spread_bias():
            x = bank()
            turned = x[:].bitcast(BF16)
            nc.tensor.transpose(turned[:, :P], bias_rows[:], ident_bf[:])
            nc.scalar.copy(out=bias[:], in_=turned[:, :16])

        def keep_warm(n):
            if n == 0:
                return
            x = bank()
            for s in range(n):
                nc.tensor.matmul(x[:], zeros[:].bitcast(BF16)[:, :P], zeros[:].bitcast(BF16), start=True, stop=True)

        def product(i, h):
            for s in (2 * h, 2 * h + 1):
                row = slice(s * D, (s + 1) * D)
                nc.vector.tensor_tensor(
                    out=v_docs[i][:, row], in0=x_docs[i][:, row].bitcast(FP8), in1=scale[:], op=ALU.mult
                )

        def turn(words, pair, order):
            x = bank()
            for s in range(2):
                base = (2 * pair + s) * 256
                for u in range(2):
                    k = (2 * s + u) * P
                    nc.tensor.transpose(x[:, k : k + P], words[:, base + u : base + 256 : 2], order[:])
            return x

        def copy(engine, out_ap, in_ap):
            if engine == "s":
                nc.scalar.copy(out=out_ap, in_=in_ap)
            else:
                nc.vector.tensor_copy(out=out_ap, in_=in_ap)

        def turn_rows(src, dst, pair, engine="s", order=ident):
            x = turn(src.bitcast(F32), pair, order)
            view = dst[:].rearrange("p n t -> p (n t)").bitcast(F32).rearrange("p (m v) -> p m v", v=8)
            copy(engine, view[:, :, 4 * pair : 4 * pair + 4], x[:].rearrange("p (v m) -> p m v", v=4))

        def quantize(dst, src):
            nc.vector.quantize_mx(out=dst[0][:].bitcast(FP8X4), scales=dst[1][:], in_=src)

        def flat(x):
            return x[:].rearrange("p n t -> p (n t)")

        def mx(acc, left, m0, right, start, stop, n0=0, n=W):
            nc.tensor.matmul_mx(
                out=acc,
                lhsT=left[0][:, m0 : m0 + P].bitcast(FP8X4),
                lhsT_scale=left[1][:, m0 : m0 + P],
                rhs=right[0][:, n0 : n0 + n].bitcast(FP8X4),
                rhs_scale=right[1][:, n0 : n0 + n],
                start=start,
                stop=stop,
            )

        def w_group(h, g, engine="v"):
            copy(
                engine,
                g_w[h][g][:].rearrange("p (t a q j) -> p t a q j", t=4, a=16, j=4),
                x_w[h][g][:].rearrange("p j (a t q) -> p t a q j", t=4, a=16),
            )

        def w_group_half(h, g, half, engine):
            lo = half * 256
            copy(
                engine,
                g_w[h][g][:].rearrange("p (t a q j) -> p t a (q j)", t=4, a=16, j=4)[:, :, half * 8 : half * 8 + 8].rearrange("p t a (q j) -> p t a q j", j=4),
                x_w[h][g][:, :, lo : lo + 256].rearrange("p j (a t q) -> p t a q j", t=4, a=8),
            )

        def w_group_pe(h, g, engines):
            for half in range(2):
                x = psum.tile([P, 2 * W], BF16, name="bank")
                for s in range(2):
                    nc.tensor.matmul(
                        x[:, s * W : (s + 1) * W].rearrange("p (a q j) -> p a q j", a=16, j=4),
                        ident_bf[:],
                        x_w[h][g][:].rearrange("p j (a t q) -> p t a q j", t=4, a=16)[:, 2 * half + s],
                        start=True,
                        stop=True,
                    )
                copy(engines[half], g_w[h][g][:, half * 2 * W : (half + 1) * 2 * W], x[:])

        planes = {}

        def match(i, g, engines="ssss"):
            pl = ring.tile([P, 4, W], BF16, name="planes", bufs=PL)
            planes[i, g] = pl
            for t in range(4):
                acc = bank()
                mx(acc[:], q_terms[g], t * P, q_docs[i], True, True)
                col = bias[:, 4 * g + t : 4 * g + t + 1]
                if engines[t] == "s":
                    nc.scalar.activation(out=pl[:, t], in_=acc[:], func=ACT.Relu, bias=col)
                else:
                    nc.vector.tensor_scalar(out=pl[:, t], in0=acc[:], scalar1=col, scalar2=0.0, op0=ALU.add, op1=ALU.max)

        def rewrite(g, engines="ssss"):
            pl = ring.tile([P, 4, W], BF16, name="planes", bufs=PL)
            planes["r", g] = pl
            for t in range(4):
                acc = bank()
                for h in range(2):
                    mx(acc[:], q_w[h][g], t * P, q_q[h], h == 0, h == 1)
                col = bias[:, 8 + 4 * g + t : 8 + 4 * g + t + 1]
                if engines[t] == "s":
                    nc.scalar.activation(out=pl[:, t], in_=acc[:], func=ACT.Identity, bias=col)
                else:
                    nc.vector.tensor_scalar(out=pl[:, t], in0=acc[:], scalar1=col, scalar2=None, op0=ALU.add)

        grouped = {}

        def new_group(key):
            if key not in grouped:
                grouped[key] = ring.tile([P, W, 4], BF16, name="grouped", align_bytes=64, bufs=5)
            return grouped[key]

        def group(key, lo, hi):
            new_group(key)
            nc.vector.tensor_copy(
                out=grouped[key][:, lo:hi].rearrange("p (c i) t -> p c t i", i=4),
                in_=planes[key][:, :, lo:hi].rearrange("p t (c i) -> p c t i", i=4),
            )

        def quantize_m(i, g, lo, hi):
            nc.vector.quantize_mx(
                out=q_m[i][g][0][:, lo:hi].bitcast(FP8X4),
                scales=q_m[i][g][1][:, lo:hi],
                in_=grouped[i, g][:, lo:hi].rearrange("p n t -> p (n t)"),
            )

        def rewrite_direct(g):
            gr = new_group(("r", g))
            shift = bias[:, 8 + 4 * g : 12 + 4 * g].unsqueeze(1).to_broadcast([P, P, 4])
            for r in range(4):
                acc = bank()
                for t in range(4):
                    for h in range(2):
                        mx(acc[:, t * P : (t + 1) * P], q_w[h][g], t * P, q_q[h], h == 0, h == 1, r * P, P)
                nc.vector.tensor_tensor(
                    out=gr[:, r * P : (r + 1) * P],
                    in0=acc[:].rearrange("p (t n) -> p n t", t=4),
                    in1=shift,
                    op=ALU.add,
                )

        def match_direct(i, g):
            gr = new_group((i, g))
            shift = bias[:, 4 * g : 4 * g + 4].unsqueeze(1).to_broadcast([P, P, 4])
            for n in range(4):
                acc = bank()
                for t in range(4):
                    mx(acc[:, t * P : (t + 1) * P], q_terms[g], t * P, q_docs[i], True, True, n * P, P)
                nc.vector.tensor_tensor(
                    out=gr[:, n * P : (n + 1) * P],
                    in0=acc[:].rearrange("p (t n) -> p n t", t=4),
                    in1=shift,
                    op=ALU.add,
                )

        def rectify(i, g):
            x = grouped[i, g][:].rearrange("p n t -> p (n t)")
            nc.vector.tensor_scalar(out=x, in0=x, scalar1=0.0, scalar2=None, op0=ALU.max)

        def quantize_r(g):
            quantize(q_r[g], flat(grouped["r", g]))

        def score(i, lo, hi, engines="ssss"):
            accs = [bank() for r in range(4)]
            for g in range(2):
                for r in range(4):
                    mx(accs[r][:, : hi - lo], q_r[g], r * P, q_m[i][g], g == 0, g == 1, lo, hi - lo)
            for r in range(4):
                res = ring.tile([P, W], F32, name="res", bufs=10)
                copy(engines[r], res[:, : hi - lo], accs[r][:, : hi - lo])
                nc.sync.dma_start(out=out_v[r][:, i * W + lo : i * W + hi], in_=res[:, : hi - lo])

        for step in ORDER:
            k, e = (step + ":").split(":")[:2]
            n = [int(x) for x in k[2:] if k[1] != 'z']
            k = k[:2]
            if k == "Zs":
                spread_scale()
            if k == "Zb":
                spread_bias()
            if k == "Zz":
                keep_warm(int(e))
            if k == "P_":
                product(n[0], n[1])
            if k == "Tt":
                turn_rows(x_terms[n[0]][:], g_terms[n[0]], n[1], e, perm)
            if k == "Tq":
                turn_rows(x_q[n[0]][:].rearrange("p r k -> p (r k)"), g_q[n[0]], n[1], e)
            if k == "Td":
                turn_rows(v_docs[n[0]][:], g_docs[n[0]], n[1], e)
            if k == "Qt":
                quantize(q_terms[n[0]], flat(g_terms[n[0]]))
            if k == "Qd":
                quantize(q_docs[n[0]], flat(g_docs[n[0]]))
            if k == "Qq":
                quantize(q_q[n[0]], flat(g_q[n[0]]))
            if k == "Iw":
                w_group(n[0], n[1], e)
            if k == "Iv":
                w_group_half(n[0], n[1], n[2], e)
            if k == "Jw":
                w_group_pe(n[0], n[1], e)
            if k == "Qw":
                quantize(q_w[n[0]][n[1]], g_w[n[0]][n[1]][:])
            if k == "M_":
                match(n[0], n[1], e)
            if k == "R_":
                rewrite(n[0], e)
            if k == "Mn":
                match_direct(n[0], n[1])
            if k == "Me":
                rectify(n[0], n[1])
            if k == "Rn":
                rewrite_direct(n[0])
            if k == "Gm":
                group((n[0], n[1]), 0, W)
            if k == "Gh":
                group((n[0], n[1]), n[2] * 256, n[2] * 256 + 256)
            if k == "Gr":
                group(("r", n[0]), 0, W)
            if k == "Qm":
                quantize_m(n[0], n[1], 0, W)
            if k == "Qh":
                quantize_m(n[0], n[1], n[2] * 256, n[2] * 256 + 256)
            if k == "Qr":
                quantize_r(n[0])
            if k == "S_":
                score(n[0], 0, W, e)
            if k == "Sh":
                score(n[0], n[1] * 256, n[1] * 256 + 256, e)
